import numpy as np
import ml_dtypes


def mxq(x, axis, fmt="e4m3"):
    dtype, down = {"e4m3": (ml_dtypes.float8_e4m3fn, 7), "e5m2": (ml_dtypes.float8_e5m2, 14)}[fmt]
    v = np.moveaxis(np.asarray(x, np.float32).astype(ml_dtypes.bfloat16).astype(np.float64), axis, -1)
    blocks = v.reshape(v.shape[:-1] + (-1, 32))
    amax = np.abs(blocks).max(-1, keepdims=True)
    byte = np.maximum(np.where(amax > 0, np.frexp(amax)[1] - 1 + 127, 0) - down, 1)
    scale = np.exp2(byte - 127.0)
    codes = (blocks / scale).astype(np.float32).astype(dtype).astype(np.float64)
    return np.moveaxis((codes * scale).reshape(v.shape), -1, axis)


WIDE = False


def mx_kscale(k, group=512):
    if not WIDE:
        return np.ones(k)
    levels = np.array([10, -10, 5, -5, 0])
    if group != 512:
        return np.exp2(np.random.permutation(np.resize(levels, k // group))).repeat(group)
    if k % 512:
        return np.exp2(np.random.permutation(np.resize(levels, k // 32))).repeat(32)
    a = np.empty((k // 512, 16))
    for p in range(k // 512):
        a[p, :8] = np.random.permutation(np.resize(levels, 8))
        for g in range(8):
            far = levels[np.abs(levels - a[p, g]) >= 10]
            a[p, g + 8] = far[np.random.randint(len(far))]
    return np.exp2(a.ravel()).repeat(32)


def f64(x):
    return np.asarray(x).astype(np.float64)


def striped(idx):
    return np.tile(np.asarray(idx).reshape(-1, 16).T, (8, 1)).astype(np.uint16)


def unstriped(offs):
    return offs[:16].T.reshape(-1).astype(np.int64)


H, KV, D, NQ, N = 2, 2, 256, 512, 1024


def setup_inputs():
    n = np.random.standard_normal
    s = mx_kscale(D, 0)[:, None]
    u = mx_kscale(N)
    t = np.random.uniform(0.5, 2.0, N) * u
    v = n((KV, N, 128))
    return {
        "qT": (n((H, D, NQ)) * s * (0.70 / np.sqrt(D))).astype(np.float32),
        "kT": (n((KV, D, N)) / s).astype(np.float32),
        "t": t.reshape(N, 1).astype(np.float32),
        "v": (v / t[:, None]).astype(np.float32),
        "mask": np.exp2(-np.abs(np.arange(NQ)[None, :] * N / NQ - np.arange(N)[:, None]) / 256.0).astype(np.float32),
        "gn": np.tile(np.random.uniform(0.5, 2.0, 128), (128, 1)).astype(np.float32),
        "og": n((H, NQ, 128)).astype(np.float32),
    }


def reference(qT, kT, t, v, mask, gn, og):
    a = mxq(f64(kT), 1, "e4m3").transpose(0, 2, 1) @ mxq(f64(qT), 1, "e4m3")
    p = a
    p = p * f64(mask)
    w = p * f64(t)
    y = mxq(w, 1, "e4m3").transpose(0, 2, 1) @ mxq(f64(v), 1, "e4m3")
    y = y / 16.0
    y = y / np.sqrt(np.mean(np.square(y), -1, keepdims=True) + 1e-5) * f64(gn)[:1]
    y = y / (1.0 + np.exp(-f64(og)))
    return y

@@ -1,0 +1,256 @@
+from contextlib import ExitStack
+
+import concourse.mybir as mybir
+
+H, D, NQ, N, E = 2, 256, 512, 1024, 128
+FLOPS = 2 * H * N * NQ * D + 2 * H * N * NQ * E
+
+F32 = mybir.dt.float32
+BF16 = mybir.dt.bfloat16
+U32 = mybir.dt.uint32
+U8 = mybir.dt.uint8
+FP8X4 = mybir.dt.float8_e4m3fn_x4
+ACT = mybir.ActivationFunctionType
+ALU = mybir.AluOpType
+
+P = 128
+PACK = 4
+ROWS = D // PACK
+PASS = P * PACK
+PASSES = N // PASS
+QB = 128
+BLOCKS = NQ // QB
+HALF = NQ // 2
+UNITS = PASSES * BLOCKS * H
+K_SPLIT = 88
+EPS = 1e-5
+
+
+def tile_rows_a_lin_mask_onorm_gate_kernel(tc, qT, kT, t, v, mask, gn, og, out):
+    nc = tc.nc
+    q_rows = qT.rearrange("h (p j) n -> (h p) j n", j=PACK)
+    k_rows = kT.rearrange("h (p j) n -> (h p) j n", j=PACK)
+    mask_rows = mask.rearrange("(g p r) n -> g p r n", g=PASSES, r=PACK)
+    v_rows = v.rearrange("h (g p r) e -> g p h (r e)", g=PASSES, r=PACK)
+    og_rows = og.rearrange("h (b p) e -> p (h b) e", p=QB)
+    out_rows = out.rearrange("h (b p) e -> p (h b) e", p=QB)
+
+    with ExitStack() as ctx:
+        keep = ctx.enter_context(tc.tile_pool(name="keep", bufs=1))
+        work = ctx.enter_context(tc.tile_pool(name="work", bufs=4))
+        psum = ctx.enter_context(tc.psum_pool(name="psum", bufs=2))
+        ctx.enter_context(tc.manual_schedule())
+
+        def kept(name, shape, dtype):
+            return keep.tile(shape, dtype, name=name, align_bytes=64)
+
+        def load(queue, name, source):
+            tile = kept(name, list(source.shape), F32)
+            queue.dma_start(out=tile[:], in_=source)
+            return tile
+
+        t_sb = load(nc.scalar, "t_sb", t.rearrange("(g p r) o -> p g (r o)", g=PASSES, r=PACK))
+        og_first = load(nc.scalar, "og_first", og_rows[:, 0:1, :])
+        q_raw = {}
+        k_raw = {}
+        v_raw = {}
+        mask_raw = {}
+        q_raw[0] = load(nc.sync, "q_raw0", q_rows[:, :, 0:HALF])
+        k_raw[0, 0] = load(nc.sync, "k_raw0", k_rows[:, :, 0:PASS])
+        mask_raw[0, 0] = load(nc.sync, "mask_raw00", mask_rows[0][:, :, 0:HALF])
+        q_raw[1] = load(nc.sync, "q_raw1", q_rows[:, :, HALF:NQ])
+        mask_raw[0, 1] = load(nc.sync, "mask_raw01", mask_rows[0][:, :, HALF:NQ])
+        k_raw[1, 0] = load(nc.sync, "k_raw10", k_rows[:, :, PASS : PASS + PASS // 2])
+        k_raw[1, P // 2] = load(nc.sync, "k_raw11", k_rows[:, :, PASS + PASS // 2 : N])
+        mask_raw[1, 0] = load(nc.sync, "mask_raw10", mask_rows[1][:, :, 0:HALF])
+        gn_sb = load(nc.sync, "gn_sb", gn)
+        og_rest = load(nc.sync, "og_rest", og_rows[:, 1 : H * BLOCKS, :])
+        v_raw[0] = load(nc.sync, "v_raw0", v_rows[0])
+        v_raw[1] = load(nc.sync, "v_raw1", v_rows[1])
+        mask_raw[1, 1] = load(nc.sync, "mask_raw11", mask_rows[1][:, :, HALF:NQ])
+
+        def quantize(name, packed, width):
+            codes = kept(name + "_codes", [P, width], U32)
+            scales = kept(name + "_scales", [P, width], U8)
+            nc.vector.quantize_mx(out=codes[:].bitcast(FP8X4), scales=scales[:], in_=packed)
+            return codes, scales
+
+        def copy_on(engine, out, in_):
+            if engine == "vector":
+                nc.vector.tensor_copy(out=out, in_=in_)
+            else:
+                nc.scalar.copy(out=out, in_=in_)
+
+        def pack_q(half, engine):
+            packed = kept("q_packed%d" % half, [P, HALF, PACK], BF16)
+            copy_on(engine, packed[:].rearrange("p (c i) j -> p c j i", i=4),
+                    q_raw[half][:].rearrange("p j (c i) -> p c j i", i=4))
+            return packed
+
+        def pack_k(packed, g, base, engine, lo, hi):
+            copy_on(engine, packed[:, :, lo:hi, :].rearrange("p r s j -> p s j r"),
+                    k_raw[g, base][:, :, PACK * (lo - base) : PACK * (hi - base)].rearrange("p j (s r) -> p s j r", r=PACK))
+
+        def pack_v(g):
+            packed = kept("v_packed%d" % g, [P, H, E, PACK], BF16)
+            nc.scalar.copy(out=packed[:].rearrange("p h (c i) r -> p h c r i", i=4),
+                           in_=v_raw[g][:].rearrange("p h (r c i) -> p h c r i", r=PACK, i=4))
+            return packed
+
+        decay = {}
+
+        def scale_mask(g, first, count, engine):
+            width = count * QB
+            half, lo = divmod(first * QB, HALF)
+            tile = kept("decay%d%d" % (g, first), [P, PACK, width], F32)
+            for r in range(PACK):
+                source = mask_raw[g, half][:, r, lo : lo + width]
+                if engine == "scalar":
+                    nc.scalar.activation(out=tile[:, r, :], in_=source, func=ACT.Copy, scale=t_sb[:, g, r : r + 1])
+                else:
+                    nc.gpsimd.tensor_scalar(out=tile[:, r, :], in0=source, scalar1=t_sb[:, g, r : r + 1],
+                                            scalar2=0.0, op0=ALU.mult, op1=ALU.add)
+            for b in range(count):
+                decay[g, first + b] = tile[:, :, b * QB : (b + 1) * QB]
+
+        q_mx = {}
+        k_mx = {}
+        v_mx = {}
+        w_mx = {}
+        banks = {}
+        w_packed = {}
+        y_banks = {}
+        inv_rms = {}
+
+        def quantize_k(g, packed):
+            for pair in range(2):
+                k_mx[g, pair] = quantize("k%d%d" % (g, pair),
+                                         packed[:, 2 * pair : 2 * pair + 2].rearrange("p r s j -> p (r s j)"), 2 * P)
+
+        def unit(u):
+            g, rest = divmod(u, BLOCKS * H)
+            b, h = divmod(rest, H)
+            return g, b, h
+
+        def scores(u):
+            g, b, h = unit(u)
+            rows = slice(ROWS * h, ROWS * (h + 1))
+            bank = psum.tile([P, PACK, QB], F32, name="scores%d" % h)
+            q_codes, q_scales = q_mx[b // 2]
+            q_cols = slice(QB * (b % 2), QB * (b % 2 + 1))
+            for r in range(PACK):
+                k_codes, k_scales = k_mx[g, r // 2]
+                k_cols = slice(P * (r % 2), P * (r % 2 + 1))
+                nc.tensor.matmul_mx(out=bank[:, r, :], lhsT=k_codes[rows, k_cols].bitcast(FP8X4),
+                                    lhsT_scale=k_scales[rows, k_cols],
+                                    rhs=q_codes[rows, q_cols].bitcast(FP8X4), rhs_scale=q_scales[rows, q_cols],
+                                    start=True, stop=True)
+            banks[u] = bank
+
+        def weigh(u):
+            g, b, h = unit(u)
+            packed = work.tile([P, QB, PACK], BF16, name="w_packed", align_bytes=64)
+            nc.vector.tensor_tensor(out=packed[:].rearrange("p (c i) r -> p c r i", i=2),
+                                    in0=banks[u][:].rearrange("p r (c i) -> p c r i", i=2),
+                                    in1=decay[g, b].rearrange("p r (c i) -> p c r i", i=2), op=ALU.mult)
+            w_packed[u] = packed
+
+        def quantize_w(u):
+            w_mx[u] = quantize("w%d" % u, w_packed[u][:].rearrange("p q r -> p (q r)"), QB)
+
+        def read_values(group):
+            bank = psum.tile([P, len(group), E], F32, name="y", bufs=4)
+            for slot, u in enumerate(group):
+                last, b, h = unit(u)
+                cols = slice(E * h, E * (h + 1))
+                for g in range(PASSES):
+                    w_codes, w_scales = w_mx[u - (last - g) * BLOCKS * H]
+                    v_codes, v_scales = v_mx[g]
+                    nc.tensor.matmul_mx(out=bank[:, slot, :], lhsT=w_codes[:].bitcast(FP8X4), lhsT_scale=w_scales[:],
+                                        rhs=v_codes[:, cols].bitcast(FP8X4), rhs_scale=v_scales[:, cols],
+                                        start=(g == 0), stop=(g == last))
+                y_banks[u] = bank[:, slot, :]
+            total = work.tile([P, len(group)], F32, name="total")
+            inv = work.tile([P, len(group)], F32, name="inv")
+            for slot, u in enumerate(group):
+                squares = work.tile([P, E], F32, name="squares")
+                nc.scalar.activation(out=squares[:], in_=y_banks[u], func=ACT.Square,
+                                     accum_out=total[:, slot : slot + 1])
+                inv_rms[u] = inv[:, slot : slot + 1]
+            nc.scalar.activation(out=inv[:], in_=total[:], func=ACT.Abs_reciprocal_sqrt,
+                                 scale=1.0 / E, bias=256.0 * EPS)
+
+        gate = kept("gate", [P, H * BLOCKS, E], F32)
+        gains = {}
+
+        def gain(pair):
+            tile = kept("gain%d" % pair, [P, 2, E], F32)
+            nc.gpsimd.tensor_tensor(out=tile[:], in0=gate[:, 2 * pair : 2 * pair + 2, :],
+                                    in1=gn_sb[:].unsqueeze(1).to_broadcast([P, 2, E]), op=ALU.mult)
+            gains[2 * pair] = tile[:, 0, :]
+            gains[2 * pair + 1] = tile[:, 1, :]
+
+        def finish(u):
+            last, b, h = unit(u)
+            result = work.tile([P, E], F32, name="result", bufs=8)
+            nc.vector.scalar_tensor_tensor(out=result[:], in0=y_banks[u], scalar=inv_rms[u],
+                                           in1=gains[h * BLOCKS + b], op0=ALU.mult, op1=ALU.mult)
+            nc.sync.dma_start(out=out_rows[:, h * BLOCKS + b, :], in_=result[:])
+
+        nc.scalar.activation(out=gate[:, 0:1, :], in_=og_first[:], func=ACT.Sigmoid)
+        q_packed = pack_q(0, "vector")
+        q_mx[0] = quantize("q0", q_packed[:].rearrange("p n j -> p (n j)"), HALF)
+        k_packed = kept("k_packed0", [P, PACK, P, PACK], BF16)
+        pack_k(k_packed, 0, 0, "vector", 0, K_SPLIT)
+        pack_k(k_packed, 0, 0, "scalar", K_SPLIT, P)
+        quantize_k(0, k_packed)
+
+        scale_mask(0, 0, 1, "scalar")
+        scale_mask(0, 1, 1, "scalar")
+        q_packed = pack_q(1, "scalar")
+        scale_mask(0, 2, 2, "gpsimd")
+        k_packed = kept("k_packed1", [P, PACK, P, PACK], BF16)
+        pack_k(k_packed, 1, 0, "scalar", 0, P // 2)
+        pack_k(k_packed, 1, P // 2, "scalar", P // 2, P)
+        scale_mask(1, 0, 1, "gpsimd")
+        scale_mask(1, 1, 1, "gpsimd")
+        nc.scalar.activation(out=gate[:, 1 : H * BLOCKS, :], in_=og_rest[:], func=ACT.Sigmoid)
+        v_packed = [pack_v(g) for g in range(PASSES)]
+        warm = kept("warm", [P, 1], F32)
+        nc.scalar.activation(out=warm[:], in_=gate[:, 0, 0:1], func=ACT.Abs_reciprocal_sqrt)
+        gain(0)
+        gain(2)
+        scale_mask(1, 2, 1, "gpsimd")
+        scale_mask(1, 3, 1, "gpsimd")
+        gain(1)
+        gain(3)
+
+        groups = {11: [8, 9, 10, 11], 13: [12, 13], 14: [14], 15: [15]}
+        issued = 0
+        ready = 4
+        for s in range(UNITS + 1):
+            while issued < min(s + 3, ready):
+                scores(issued)
+                issued = issued + 1
+            if s < UNITS:
+                weigh(s)
+            else:
+                finish(8)
+            if s == 2:
+                q_mx[1] = quantize("q1", q_packed[:].rearrange("p n j -> p (n j)"), HALF)
+                ready = 8
+            if s == 6:
+                quantize_k(1, k_packed)
+                ready = UNITS
+            if s in (10, 12):
+                g = (s - 10) // 2
+                v_mx[g] = quantize("v%d" % g, v_packed[g][:].rearrange("p h e r -> p (h e r)"), H * E)
+            while issued < min(s + 4, ready):
+                scores(issued)
+                issued = issued + 1
+            if s >= 1:
+                quantize_w(s - 1)
+            if s - 1 in groups:
+                read_values(groups[s - 1])
+        for u in range(9, UNITS):
+            finish(u)

@@ -22,7 +22,6 @@ QB = 128
 BLOCKS = NQ // QB
 HALF = NQ // 2
 UNITS = PASSES * BLOCKS * H
-K_SPLIT = 88
 EPS = 1e-5
 
 
@@ -50,24 +49,32 @@ def tile_rows_a_lin_mask_onorm_gate_kernel(tc, qT, kT, t, v, mask, gn, og, out):
             return tile
 
         t_sb = load(nc.scalar, "t_sb", t.rearrange("(g p r) o -> p g (r o)", g=PASSES, r=PACK))
-        og_first = load(nc.scalar, "og_first", og_rows[:, 0:1, :])
         q_raw = {}
         k_raw = {}
         v_raw = {}
         mask_raw = {}
-        q_raw[0] = load(nc.sync, "q_raw0", q_rows[:, :, 0:HALF])
-        k_raw[0, 0] = load(nc.sync, "k_raw0", k_rows[:, :, 0:PASS])
-        mask_raw[0, 0] = load(nc.sync, "mask_raw00", mask_rows[0][:, :, 0:HALF])
-        q_raw[1] = load(nc.sync, "q_raw1", q_rows[:, :, HALF:NQ])
-        mask_raw[0, 1] = load(nc.sync, "mask_raw01", mask_rows[0][:, :, HALF:NQ])
-        k_raw[1, 0] = load(nc.sync, "k_raw10", k_rows[:, :, PASS : PASS + PASS // 2])
-        k_raw[1, P // 2] = load(nc.sync, "k_raw11", k_rows[:, :, PASS + PASS // 2 : N])
-        mask_raw[1, 0] = load(nc.sync, "mask_raw10", mask_rows[1][:, :, 0:HALF])
-        gn_sb = load(nc.sync, "gn_sb", gn)
+
+        def load_q(first, count):
+            q_raw[first] = load(nc.sync, "q_raw%d" % first, q_rows[:, :, QB * first : QB * (first + count)])
+
+        def load_k(g):
+            k_raw[g] = load(nc.sync, "k_raw%d" % g, k_rows[:, :, PASS * g : PASS * (g + 1)])
+
+        def load_mask(g, first, count):
+            tile = load(nc.sync, "mask_raw%d%d" % (g, first), mask_rows[g][:, :, QB * first : QB * (first + count)])
+            mask_raw[g, first] = tile
+
+        og_first = load(nc.scalar, "og_first", og_rows[:, 0:1, :])
+        load_k(0)
+        for first in (0, 2):
+            load_q(first, 2)
+            load_mask(0, first, 2)
+        load_k(1)
+        for g in range(PASSES):
+            load_mask(1, 2 * g, 2)
+            v_raw[g] = load(nc.sync, "v_raw%d" % g, v_rows[g])
         og_rest = load(nc.sync, "og_rest", og_rows[:, 1 : H * BLOCKS, :])
-        v_raw[0] = load(nc.sync, "v_raw0", v_rows[0])
-        v_raw[1] = load(nc.sync, "v_raw1", v_rows[1])
-        mask_raw[1, 1] = load(nc.sync, "mask_raw11", mask_rows[1][:, :, HALF:NQ])
+        gn_sb = load(nc.sync, "gn_sb", gn)
 
         def quantize(name, packed, width):
             codes = kept(name + "_codes", [P, width], U32)
@@ -81,15 +88,22 @@ def tile_rows_a_lin_mask_onorm_gate_kernel(tc, qT, kT, t, v, mask, gn, og, out):
             else:
                 nc.scalar.copy(out=out, in_=in_)
 
-        def pack_q(half, engine):
-            packed = kept("q_packed%d" % half, [P, HALF, PACK], BF16)
+        def pack_q(first, count, engine):
+            packed = kept("q_packed%d" % first, [P, count * QB, PACK], BF16)
             copy_on(engine, packed[:].rearrange("p (c i) j -> p c j i", i=4),
-                    q_raw[half][:].rearrange("p j (c i) -> p c j i", i=4))
+                    q_raw[first][:].rearrange("p j (c i) -> p c j i", i=4))
             return packed
 
-        def pack_k(packed, g, base, engine, lo, hi):
-            copy_on(engine, packed[:, :, lo:hi, :].rearrange("p r s j -> p s j r"),
-                    k_raw[g, base][:, :, PACK * (lo - base) : PACK * (hi - base)].rearrange("p j (s r) -> p s j r", r=PACK))
+        def quantize_q(first, count, packed):
+            codes, scales = quantize("q%d" % first, packed[:].rearrange("p n j -> p (n j)"), count * QB)
+            for b in range(count):
+                q_mx[first + b] = (codes, scales, slice(QB * b, QB * (b + 1)))
+
+        def pack_k(g, pair, engine):
+            packed = kept("k_packed%d%d" % (g, pair), [P, 2, P, PACK], BF16)
+            copy_on(engine, packed[:].rearrange("p r s j -> p s j r"),
+                    k_raw[g][:].rearrange("p j (s r) -> p s j r", r=PACK)[:, :, :, 2 * pair : 2 * pair + 2])
+            k_packed[g, pair] = packed
 
         def pack_v(g):
             packed = kept("v_packed%d" % g, [P, H, E, PACK], BF16)
@@ -98,21 +112,20 @@ def tile_rows_a_lin_mask_onorm_gate_kernel(tc, qT, kT, t, v, mask, gn, og, out):
             return packed
 
         decay = {}
+        power = kept("power", [P, 4], F32)
+        nc.gpsimd.memset(power[:], -0.5)
 
-        def scale_mask(g, first, count, engine):
-            width = count * QB
-            half, lo = divmod(first * QB, HALF)
-            tile = kept("decay%d%d" % (g, first), [P, PACK, width], F32)
+        def scale_mask(g, first, count):
+            chunk = first - first % 2
+            cols = slice(QB * (first - chunk), QB * (first - chunk + count))
+            tile = kept("decay%d%d" % (g, first), [P, PACK, count * QB], F32)
             for r in range(PACK):
-                source = mask_raw[g, half][:, r, lo : lo + width]
-                if engine == "scalar":
-                    nc.scalar.activation(out=tile[:, r, :], in_=source, func=ACT.Copy, scale=t_sb[:, g, r : r + 1])
-                else:
-                    nc.gpsimd.tensor_scalar(out=tile[:, r, :], in0=source, scalar1=t_sb[:, g, r : r + 1],
-                                            scalar2=0.0, op0=ALU.mult, op1=ALU.add)
+                nc.scalar.activation(out=tile[:, r, :], in_=mask_raw[g, chunk][:, r, cols], func=ACT.Copy,
+                                     scale=t_sb[:, g, r : r + 1])
             for b in range(count):
                 decay[g, first + b] = tile[:, :, b * QB : (b + 1) * QB]
 
+        k_packed = {}
         q_mx = {}
         k_mx = {}
         v_mx = {}
@@ -122,10 +135,8 @@ def tile_rows_a_lin_mask_onorm_gate_kernel(tc, qT, kT, t, v, mask, gn, og, out):
         y_banks = {}
         inv_rms = {}
 
-        def quantize_k(g, packed):
-            for pair in range(2):
-                k_mx[g, pair] = quantize("k%d%d" % (g, pair),
-                                         packed[:, 2 * pair : 2 * pair + 2].rearrange("p r s j -> p (r s j)"), 2 * P)
+        def quantize_k(g, pair):
+            k_mx[g, pair] = quantize("k%d%d" % (g, pair), k_packed[g, pair][:].rearrange("p r s j -> p (r s j)"), 2 * P)
 
         def unit(u):
             g, rest = divmod(u, BLOCKS * H)
@@ -136,8 +147,7 @@ def tile_rows_a_lin_mask_onorm_gate_kernel(tc, qT, kT, t, v, mask, gn, og, out):
             g, b, h = unit(u)
             rows = slice(ROWS * h, ROWS * (h + 1))
             bank = psum.tile([P, PACK, QB], F32, name="scores%d" % h)
-            q_codes, q_scales = q_mx[b // 2]
-            q_cols = slice(QB * (b % 2), QB * (b % 2 + 1))
+            q_codes, q_scales, q_cols = q_mx[b]
             for r in range(PACK):
                 k_codes, k_scales = k_mx[g, r // 2]
                 k_cols = slice(P * (r % 2), P * (r % 2 + 1))
@@ -177,55 +187,42 @@ def tile_rows_a_lin_mask_onorm_gate_kernel(tc, qT, kT, t, v, mask, gn, og, out):
                 nc.scalar.activation(out=squares[:], in_=y_banks[u], func=ACT.Square,
                                      accum_out=total[:, slot : slot + 1])
                 inv_rms[u] = inv[:, slot : slot + 1]
-            nc.scalar.activation(out=inv[:], in_=total[:], func=ACT.Abs_reciprocal_sqrt,
-                                 scale=1.0 / E, bias=256.0 * EPS)
+            mean = work.tile([P, len(group)], F32, name="mean")
+            nc.gpsimd.tensor_scalar(out=mean[:], in0=total[:], scalar1=1.0 / E, scalar2=256.0 * EPS,
+                                    op0=ALU.mult, op1=ALU.add)
+            nc.gpsimd.tensor_tensor(out=inv[:], in0=mean[:], in1=power[:, 0 : len(group)], op=ALU.pow)
 
         gate = kept("gate", [P, H * BLOCKS, E], F32)
-        gains = {}
-
-        def gain(pair):
-            tile = kept("gain%d" % pair, [P, 2, E], F32)
-            nc.gpsimd.tensor_tensor(out=tile[:], in0=gate[:, 2 * pair : 2 * pair + 2, :],
-                                    in1=gn_sb[:].unsqueeze(1).to_broadcast([P, 2, E]), op=ALU.mult)
-            gains[2 * pair] = tile[:, 0, :]
-            gains[2 * pair + 1] = tile[:, 1, :]
+        gains = kept("gains", [P, H * BLOCKS, E], F32)
 
         def finish(u):
             last, b, h = unit(u)
             result = work.tile([P, E], F32, name="result", bufs=8)
             nc.vector.scalar_tensor_tensor(out=result[:], in0=y_banks[u], scalar=inv_rms[u],
-                                           in1=gains[h * BLOCKS + b], op0=ALU.mult, op1=ALU.mult)
+                                           in1=gains[:, h * BLOCKS + b, :], op0=ALU.mult, op1=ALU.mult)
             nc.sync.dma_start(out=out_rows[:, h * BLOCKS + b, :], in_=result[:])
 
         nc.scalar.activation(out=gate[:, 0:1, :], in_=og_first[:], func=ACT.Sigmoid)
-        q_packed = pack_q(0, "vector")
-        q_mx[0] = quantize("q0", q_packed[:].rearrange("p n j -> p (n j)"), HALF)
-        k_packed = kept("k_packed0", [P, PACK, P, PACK], BF16)
-        pack_k(k_packed, 0, 0, "vector", 0, K_SPLIT)
-        pack_k(k_packed, 0, 0, "scalar", K_SPLIT, P)
-        quantize_k(0, k_packed)
+        pack_k(0, 0, "vector")
+        pack_k(0, 1, "scalar")
+        quantize_k(0, 0)
+        q_first = pack_q(0, 2, "vector")
+        quantize_k(0, 1)
+        quantize_q(0, 2, q_first)
 
-        scale_mask(0, 0, 1, "scalar")
-        scale_mask(0, 1, 1, "scalar")
-        q_packed = pack_q(1, "scalar")
-        scale_mask(0, 2, 2, "gpsimd")
-        k_packed = kept("k_packed1", [P, PACK, P, PACK], BF16)
-        pack_k(k_packed, 1, 0, "scalar", 0, P // 2)
-        pack_k(k_packed, 1, P // 2, "scalar", P // 2, P)
-        scale_mask(1, 0, 1, "gpsimd")
-        scale_mask(1, 1, 1, "gpsimd")
+        scale_mask(0, 0, 1)
+        scale_mask(0, 1, 1)
+        q_rest = pack_q(2, 2, "scalar")
+        scale_mask(0, 2, 2)
+        pack_k(1, 1, "scalar")
+        scale_mask(1, 0, 1)
+        scale_mask(1, 1, 1)
+        v_packed = [pack_v(0)]
+        scale_mask(1, 2, 2)
+        v_packed.append(pack_v(1))
         nc.scalar.activation(out=gate[:, 1 : H * BLOCKS, :], in_=og_rest[:], func=ACT.Sigmoid)
-        v_packed = [pack_v(g) for g in range(PASSES)]
-        warm = kept("warm", [P, 1], F32)
-        nc.scalar.activation(out=warm[:], in_=gate[:, 0, 0:1], func=ACT.Abs_reciprocal_sqrt)
-        gain(0)
-        gain(2)
-        scale_mask(1, 2, 1, "gpsimd")
-        scale_mask(1, 3, 1, "gpsimd")
-        gain(1)
-        gain(3)
 
-        groups = {11: [8, 9, 10, 11], 13: [12, 13], 14: [14], 15: [15]}
+        groups = {12: [8, 9, 10, 11], 13: [12, 13], 14: [14], 15: [15]}
         issued = 0
         ready = 4
         for s in range(UNITS + 1):
@@ -235,15 +232,19 @@ def tile_rows_a_lin_mask_onorm_gate_kernel(tc, qT, kT, t, v, mask, gn, og, out):
             if s < UNITS:
                 weigh(s)
             else:
-                finish(8)
+                nc.vector.tensor_tensor(out=gains[:, 0:1, :], in0=gate[:, 0:1, :],
+                                        in1=gn_sb[:].unsqueeze(1), op=ALU.mult)
             if s == 2:
-                q_mx[1] = quantize("q1", q_packed[:].rearrange("p n j -> p (n j)"), HALF)
+                quantize_q(2, 2, q_rest)
                 ready = 8
+            if s == 5:
+                pack_k(1, 0, "vector")
             if s == 6:
-                quantize_k(1, k_packed)
+                quantize_k(1, 0)
+                quantize_k(1, 1)
                 ready = UNITS
-            if s in (10, 12):
-                g = (s - 10) // 2
+            if s in (10, 13):
+                g = (s - 10) // 3
                 v_mx[g] = quantize("v%d" % g, v_packed[g][:].rearrange("p h e r -> p (h e r)"), H * E)
             while issued < min(s + 4, ready):
                 scores(issued)
@@ -252,5 +253,7 @@ def tile_rows_a_lin_mask_onorm_gate_kernel(tc, qT, kT, t, v, mask, gn, og, out):
                 quantize_w(s - 1)
             if s - 1 in groups:
                 read_values(groups[s - 1])
-        for u in range(9, UNITS):
+        nc.vector.tensor_tensor(out=gains[:, 1:, :], in0=gate[:, 1:, :],
+                                in1=gn_sb[:].unsqueeze(1).to_broadcast([P, H * BLOCKS - 1, E]), op=ALU.mult)
+        for u in range(8, UNITS):
             finish(u)

@@ -23,6 +23,7 @@ BLOCKS = NQ // QB
 HALF = NQ // 2
 UNITS = PASSES * BLOCKS * H
 EPS = 1e-5
+ROOTS_FROM = 4
 
 
 def tile_rows_a_lin_mask_onorm_gate_kernel(tc, qT, kT, t, v, mask, gn, og, out):
@@ -55,26 +56,32 @@ def tile_rows_a_lin_mask_onorm_gate_kernel(tc, qT, kT, t, v, mask, gn, og, out):
         mask_raw = {}
 
         def load_q(first, count):
-            q_raw[first] = load(nc.sync, "q_raw%d" % first, q_rows[:, :, QB * first : QB * (first + count)])
+            tile = load(nc.sync, "q_raw%d" % first, q_rows[:, :, QB * first : QB * (first + count)])
+            for b in range(count):
+                q_raw[first + b] = (tile, QB * b)
 
         def load_k(g):
             k_raw[g] = load(nc.sync, "k_raw%d" % g, k_rows[:, :, PASS * g : PASS * (g + 1)])
 
         def load_mask(g, first, count):
             tile = load(nc.sync, "mask_raw%d%d" % (g, first), mask_rows[g][:, :, QB * first : QB * (first + count)])
-            mask_raw[g, first] = tile
+            for b in range(count):
+                mask_raw[g, first + b] = (tile, QB * b)
 
         og_first = load(nc.scalar, "og_first", og_rows[:, 0:1, :])
-        load_k(0)
-        for first in (0, 2):
-            load_q(first, 2)
-            load_mask(0, first, 2)
-        load_k(1)
-        for g in range(PASSES):
-            load_mask(1, 2 * g, 2)
+        def load_v(g):
             v_raw[g] = load(nc.sync, "v_raw%d" % g, v_rows[g])
-        og_rest = load(nc.sync, "og_rest", og_rows[:, 1 : H * BLOCKS, :])
+        load_k(0)
+        load_q(0, 4)
+        load_mask(0, 0, 2)
+        load_mask(0, 2, 2)
         gn_sb = load(nc.sync, "gn_sb", gn)
+        og_rest = load(nc.sync, "og_rest", og_rows[:, 1 : H * BLOCKS, :])
+        load_k(1)
+        load_mask(1, 0, 2)
+        load_v(0)
+        load_v(1)
+        load_mask(1, 2, 2)
 
         def quantize(name, packed, width):
             codes = kept(name + "_codes", [P, width], U32)
@@ -91,7 +98,7 @@ def tile_rows_a_lin_mask_onorm_gate_kernel(tc, qT, kT, t, v, mask, gn, og, out):
         def pack_q(first, count, engine):
             packed = kept("q_packed%d" % first, [P, count * QB, PACK], BF16)
             copy_on(engine, packed[:].rearrange("p (c i) j -> p c j i", i=4),
-                    q_raw[first][:].rearrange("p j (c i) -> p c j i", i=4))
+                    q_raw[first][0][:, :, q_raw[first][1] : q_raw[first][1] + QB * count].rearrange("p j (c i) -> p c j i", i=4))
             return packed
 
         def quantize_q(first, count, packed):
@@ -99,11 +106,11 @@ def tile_rows_a_lin_mask_onorm_gate_kernel(tc, qT, kT, t, v, mask, gn, og, out):
             for b in range(count):
                 q_mx[first + b] = (codes, scales, slice(QB * b, QB * (b + 1)))
 
-        def pack_k(g, pair, engine):
-            packed = kept("k_packed%d%d" % (g, pair), [P, 2, P, PACK], BF16)
-            copy_on(engine, packed[:].rearrange("p r s j -> p s j r"),
-                    k_raw[g][:].rearrange("p j (s r) -> p s j r", r=PACK)[:, :, :, 2 * pair : 2 * pair + 2])
-            k_packed[g, pair] = packed
+        def pack_k(g, pair, engine, lo=0, hi=P):
+            if (g, pair) not in k_packed:
+                k_packed[g, pair] = kept("k_packed%d%d" % (g, pair), [P, 2, P, PACK], BF16)
+            copy_on(engine, k_packed[g, pair][:, :, lo:hi, :].rearrange("p r s j -> p s j r"),
+                    k_raw[g][:].rearrange("p j (s r) -> p s j r", r=PACK)[:, lo:hi, :, 2 * pair : 2 * pair + 2])
 
         def pack_v(g):
             packed = kept("v_packed%d" % g, [P, H, E, PACK], BF16)
@@ -112,20 +119,26 @@ def tile_rows_a_lin_mask_onorm_gate_kernel(tc, qT, kT, t, v, mask, gn, og, out):
             return packed
 
         decay = {}
-        power = kept("power", [P, 4], F32)
-        nc.gpsimd.memset(power[:], -0.5)
 
-        def scale_mask(g, first, count):
-            chunk = first - first % 2
-            cols = slice(QB * (first - chunk), QB * (first - chunk + count))
+        def scale_mask(g, first, count, engine="scalar"):
+            source, lo = mask_raw[g, first]
+            cols = slice(lo, lo + QB * count)
             tile = kept("decay%d%d" % (g, first), [P, PACK, count * QB], F32)
             for r in range(PACK):
-                nc.scalar.activation(out=tile[:, r, :], in_=mask_raw[g, chunk][:, r, cols], func=ACT.Copy,
-                                     scale=t_sb[:, g, r : r + 1])
+                if engine == "scalar":
+                    nc.scalar.activation(out=tile[:, r, :], in_=source[:, r, cols], func=ACT.Copy,
+                                         scale=t_sb[:, g, r : r + 1])
+                elif engine == "vector":
+                    nc.vector.tensor_scalar(out=tile[:, r, :], in0=source[:, r, cols], scalar1=t_sb[:, g, r : r + 1],
+                                            scalar2=None, op0=ALU.mult)
+                else:
+                    nc.gpsimd.tensor_scalar(out=tile[:, r, :], in0=source[:, r, cols], scalar1=t_sb[:, g, r : r + 1],
+                                            scalar2=0.0, op0=ALU.mult, op1=ALU.add)
             for b in range(count):
                 decay[g, first + b] = tile[:, :, b * QB : (b + 1) * QB]
 
         k_packed = {}
+        pending = []
         q_mx = {}
         k_mx = {}
         v_mx = {}
@@ -159,7 +172,7 @@ def tile_rows_a_lin_mask_onorm_gate_kernel(tc, qT, kT, t, v, mask, gn, og, out):
 
         def weigh(u):
             g, b, h = unit(u)
-            packed = work.tile([P, QB, PACK], BF16, name="w_packed", align_bytes=64)
+            packed = work.tile([P, QB, PACK], BF16, name="w_packed", align_bytes=64, bufs=6)
             nc.vector.tensor_tensor(out=packed[:].rearrange("p (c i) r -> p c r i", i=2),
                                     in0=banks[u][:].rearrange("p r (c i) -> p c r i", i=2),
                                     in1=decay[g, b].rearrange("p r (c i) -> p c r i", i=2), op=ALU.mult)
@@ -168,32 +181,44 @@ def tile_rows_a_lin_mask_onorm_gate_kernel(tc, qT, kT, t, v, mask, gn, og, out):
         def quantize_w(u):
             w_mx[u] = quantize("w%d" % u, w_packed[u][:].rearrange("p q r -> p (q r)"), QB)
 
-        def read_values(group):
-            bank = psum.tile([P, len(group), E], F32, name="y", bufs=4)
-            for slot, u in enumerate(group):
-                last, b, h = unit(u)
-                cols = slice(E * h, E * (h + 1))
-                for g in range(PASSES):
-                    w_codes, w_scales = w_mx[u - (last - g) * BLOCKS * H]
-                    v_codes, v_scales = v_mx[g]
-                    nc.tensor.matmul_mx(out=bank[:, slot, :], lhsT=w_codes[:].bitcast(FP8X4), lhsT_scale=w_scales[:],
-                                        rhs=v_codes[:, cols].bitcast(FP8X4), rhs_scale=v_scales[:, cols],
-                                        start=(g == 0), stop=(g == last))
-                y_banks[u] = bank[:, slot, :]
-            total = work.tile([P, len(group)], F32, name="total")
-            inv = work.tile([P, len(group)], F32, name="inv")
-            for slot, u in enumerate(group):
-                squares = work.tile([P, E], F32, name="squares")
-                nc.scalar.activation(out=squares[:], in_=y_banks[u], func=ACT.Square,
-                                     accum_out=total[:, slot : slot + 1])
-                inv_rms[u] = inv[:, slot : slot + 1]
-            mean = work.tile([P, len(group)], F32, name="mean")
-            nc.gpsimd.tensor_scalar(out=mean[:], in0=total[:], scalar1=1.0 / E, scalar2=256.0 * EPS,
-                                    op0=ALU.mult, op1=ALU.add)
-            nc.gpsimd.tensor_tensor(out=inv[:], in0=mean[:], in1=power[:, 0 : len(group)], op=ALU.pow)
+        totals = kept("totals", [P, H * BLOCKS], F32)
+        inverse = kept("inverse", [P, H * BLOCKS], F32)
+        y_tiles = [psum.tile([P, 3, E], F32, name="y", bufs=4) for bank in range(4)]
+
+        def roots(lo, hi):
+            nc.scalar.activation(out=inverse[:, lo:hi], in_=totals[:, lo:hi], func=ACT.Abs_reciprocal_sqrt,
+                                 scale=1.0 / E, bias=256.0 * EPS)
+
+        def read_values(u):
+            last, b, h = unit(u)
+            n = u - H * BLOCKS
+            slot, bank = (0, H + h) if b == BLOCKS - 1 else (b, h)
+            y = y_tiles[bank][:, slot, :]
+            cols = slice(E * h, E * (h + 1))
+            for g in range(PASSES):
+                w_codes, w_scales = w_mx[u - (last - g) * BLOCKS * H]
+                v_codes, v_scales = v_mx[g]
+                nc.tensor.matmul_mx(out=y, lhsT=w_codes[:].bitcast(FP8X4), lhsT_scale=w_scales[:],
+                                    rhs=v_codes[:, cols].bitcast(FP8X4), rhs_scale=v_scales[:, cols],
+                                    start=(g == 0), stop=(g == last))
+            y_banks[u] = y
+            squares = work.tile([P, E], F32, name="squares")
+            nc.scalar.activation(out=squares[:], in_=y, func=ACT.Square, accum_out=totals[:, n : n + 1])
+            inv_rms[u] = inverse[:, n : n + 1]
+            if n == ROOTS_FROM:
+                roots(0, n)
+            elif n > ROOTS_FROM:
+                roots(n - 1, n)
+            if u == UNITS - 1:
+                roots(n, n + 1)
 
         gate = kept("gate", [P, H * BLOCKS, E], F32)
         gains = kept("gains", [P, H * BLOCKS, E], F32)
+
+        def gain(engine, lo, count):
+            tiles = slice(lo, lo + count)
+            engine.tensor_tensor(out=gains[:, tiles, :], in0=gate[:, tiles, :],
+                                 in1=gn_sb[:].unsqueeze(1).to_broadcast([P, count, E]), op=ALU.mult)
 
         def finish(u):
             last, b, h = unit(u)
@@ -206,25 +231,34 @@ def tile_rows_a_lin_mask_onorm_gate_kernel(tc, qT, kT, t, v, mask, gn, og, out):
         pack_k(0, 0, "vector")
         pack_k(0, 1, "scalar")
         quantize_k(0, 0)
-        q_first = pack_q(0, 2, "vector")
         quantize_k(0, 1)
-        quantize_q(0, 2, q_first)
-
-        scale_mask(0, 0, 1)
-        scale_mask(0, 1, 1)
+        q_first = pack_q(0, 1, "vector")
+        q_second = pack_q(1, 1, "vector")
         q_rest = pack_q(2, 2, "scalar")
+        quantize_q(0, 1, q_first)
+        quantize_q(1, 1, q_second)
+        scale_mask(0, 0, 1, "vector")
+        quantize_q(2, 2, q_rest)
+        scale_mask(0, 1, 1)
         scale_mask(0, 2, 2)
-        pack_k(1, 1, "scalar")
+        for h in range(H):
+            lo = max(1, BLOCKS * h)
+            hi = BLOCKS * (h + 1)
+            nc.scalar.activation(out=gate[:, lo:hi, :], in_=og_rest[:, lo - 1 : hi - 1, :], func=ACT.Sigmoid)
+            if h == 0:
+                gain(nc.gpsimd, 0, BLOCKS)
+        warm = kept("warm", [P, 1], F32)
+        nc.scalar.activation(out=warm[:], in_=gate[:, 0, 0:1], func=ACT.Abs_reciprocal_sqrt)
+        pack_k(1, 1, "scalar", 0, 64)
         scale_mask(1, 0, 1)
         scale_mask(1, 1, 1)
-        v_packed = [pack_v(0)]
-        scale_mask(1, 2, 2)
-        v_packed.append(pack_v(1))
-        nc.scalar.activation(out=gate[:, 1 : H * BLOCKS, :], in_=og_rest[:], func=ACT.Sigmoid)
+        v_packed = [pack_v(0), pack_v(1)]
+        scale_mask(1, 2, 1)
+        scale_mask(1, 3, 1)
 
-        groups = {12: [8, 9, 10, 11], 13: [12, 13], 14: [14], 15: [15]}
+        groups = {10: [8, 9, 10], 11: [11], 12: [12], 13: [13], 14: [14], 15: [15]}
         issued = 0
-        ready = 4
+        ready = 8
         for s in range(UNITS + 1):
             while issued < min(s + 3, ready):
                 scores(issued)
@@ -232,28 +266,27 @@ def tile_rows_a_lin_mask_onorm_gate_kernel(tc, qT, kT, t, v, mask, gn, og, out):
             if s < UNITS:
                 weigh(s)
             else:
-                nc.vector.tensor_tensor(out=gains[:, 0:1, :], in0=gate[:, 0:1, :],
-                                        in1=gn_sb[:].unsqueeze(1), op=ALU.mult)
-            if s == 2:
-                quantize_q(2, 2, q_rest)
-                ready = 8
-            if s == 5:
+                gain(nc.vector, BLOCKS, 1)
+            if s == 7:
                 pack_k(1, 0, "vector")
-            if s == 6:
+                pack_k(1, 1, "vector", 64, P)
                 quantize_k(1, 0)
                 quantize_k(1, 1)
                 ready = UNITS
-            if s in (10, 13):
-                g = (s - 10) // 3
-                v_mx[g] = quantize("v%d" % g, v_packed[g][:].rearrange("p h e r -> p (h e r)"), H * E)
+                for u in range(3, 6):
+                    quantize_w(u)
+            for g in range(PASSES):
+                if s == (10, 11)[g]:
+                    v_mx[g] = quantize("v%d" % g, v_packed[g][:].rearrange("p h e r -> p (h e r)"), H * E)
             while issued < min(s + 4, ready):
                 scores(issued)
                 issued = issued + 1
-            if s >= 1:
+            if s >= 1 and not 3 <= s - 1 < 6:
                 quantize_w(s - 1)
-            if s - 1 in groups:
-                read_values(groups[s - 1])
-        nc.vector.tensor_tensor(out=gains[:, 1:, :], in0=gate[:, 1:, :],
-                                in1=gn_sb[:].unsqueeze(1).to_broadcast([P, H * BLOCKS - 1, E]), op=ALU.mult)
-        for u in range(8, UNITS):
+            for u in groups.get(s - 1, []):
+                read_values(u)
+        for b in range(BLOCKS - 1):
+            finish(UNITS // 2 + H * b)
+            gain(nc.vector, BLOCKS + b + 1, 1)
+        for u in (9, 11, 13, 14, 15):
             finish(u)

from contextlib import ExitStack

import concourse.mybir as mybir

H, D, NQ, N, E = 2, 256, 512, 1024, 128
FLOPS = 2 * H * N * NQ * D + 2 * H * N * NQ * E

F32 = mybir.dt.float32
BF16 = mybir.dt.bfloat16
U32 = mybir.dt.uint32
U8 = mybir.dt.uint8
FP8X4 = mybir.dt.float8_e4m3fn_x4
ACT = mybir.ActivationFunctionType
ALU = mybir.AluOpType

P = 128
PACK = 4
ROWS = D // PACK
PASS = P * PACK
PASSES = N // PASS
QB = 128
BLOCKS = NQ // QB
HALF = NQ // 2
UNITS = PASSES * BLOCKS * H
EPS = 1e-5
ROOTS_FROM = 4


def tile_rows_a_lin_mask_onorm_gate_kernel(tc, qT, kT, t, v, mask, gn, og, out):
    nc = tc.nc
    q_rows = qT.rearrange("h (p j) n -> (h p) j n", j=PACK)
    k_rows = kT.rearrange("h (p j) n -> (h p) j n", j=PACK)
    mask_rows = mask.rearrange("(g p r) n -> g p r n", g=PASSES, r=PACK)
    v_rows = v.rearrange("h (g p r) e -> g p h (r e)", g=PASSES, r=PACK)
    og_rows = og.rearrange("h (b p) e -> p (h b) e", p=QB)
    out_rows = out.rearrange("h (b p) e -> p (h b) e", p=QB)

    with ExitStack() as ctx:
        keep = ctx.enter_context(tc.tile_pool(name="keep", bufs=1))
        work = ctx.enter_context(tc.tile_pool(name="work", bufs=4))
        psum = ctx.enter_context(tc.psum_pool(name="psum", bufs=2))
        ctx.enter_context(tc.manual_schedule())

        def kept(name, shape, dtype):
            return keep.tile(shape, dtype, name=name, align_bytes=64)

        def load(queue, name, source):
            tile = kept(name, list(source.shape), F32)
            queue.dma_start(out=tile[:], in_=source)
            return tile

        t_sb = load(nc.scalar, "t_sb", t.rearrange("(g p r) o -> p g (r o)", g=PASSES, r=PACK))
        q_raw = {}
        k_raw = {}
        v_raw = {}
        mask_raw = {}

        def load_q(first, count):
            tile = load(nc.sync, "q_raw%d" % first, q_rows[:, :, QB * first : QB * (first + count)])
            for b in range(count):
                q_raw[first + b] = (tile, QB * b)

        def load_k(g):
            k_raw[g] = load(nc.sync, "k_raw%d" % g, k_rows[:, :, PASS * g : PASS * (g + 1)])

        def load_mask(g, first, count):
            tile = load(nc.sync, "mask_raw%d%d" % (g, first), mask_rows[g][:, :, QB * first : QB * (first + count)])
            for b in range(count):
                mask_raw[g, first + b] = (tile, QB * b)

        og_first = load(nc.scalar, "og_first", og_rows[:, 0:1, :])
        def load_v(g):
            v_raw[g] = load(nc.sync, "v_raw%d" % g, v_rows[g])
        load_k(0)
        load_q(0, 4)
        load_mask(0, 0, 2)
        load_mask(0, 2, 2)
        gn_sb = load(nc.sync, "gn_sb", gn)
        og_rest = load(nc.sync, "og_rest", og_rows[:, 1 : H * BLOCKS, :])
        load_k(1)
        load_mask(1, 0, 2)
        load_v(0)
        load_v(1)
        load_mask(1, 2, 2)

        def quantize(name, packed, width):
            codes = kept(name + "_codes", [P, width], U32)
            scales = kept(name + "_scales", [P, width], U8)
            nc.vector.quantize_mx(out=codes[:].bitcast(FP8X4), scales=scales[:], in_=packed)
            return codes, scales

        def copy_on(engine, out, in_):
            if engine == "vector":
                nc.vector.tensor_copy(out=out, in_=in_)
            else:
                nc.scalar.copy(out=out, in_=in_)

        def pack_q(first, count, engine):
            packed = kept("q_packed%d" % first, [P, count * QB, PACK], BF16)
            copy_on(engine, packed[:].rearrange("p (c i) j -> p c j i", i=4),
                    q_raw[first][0][:, :, q_raw[first][1] : q_raw[first][1] + QB * count].rearrange("p j (c i) -> p c j i", i=4))
            return packed

        def quantize_q(first, count, packed):
            codes, scales = quantize("q%d" % first, packed[:].rearrange("p n j -> p (n j)"), count * QB)
            for b in range(count):
                q_mx[first + b] = (codes, scales, slice(QB * b, QB * (b + 1)))

        def pack_k(g, pair, engine, lo=0, hi=P):
            if (g, pair) not in k_packed:
                k_packed[g, pair] = kept("k_packed%d%d" % (g, pair), [P, 2, P, PACK], BF16)
            copy_on(engine, k_packed[g, pair][:, :, lo:hi, :].rearrange("p r s j -> p s j r"),
                    k_raw[g][:].rearrange("p j (s r) -> p s j r", r=PACK)[:, lo:hi, :, 2 * pair : 2 * pair + 2])

        def pack_v(g):
            packed = kept("v_packed%d" % g, [P, H, E, PACK], BF16)
            nc.scalar.copy(out=packed[:].rearrange("p h (c i) r -> p h c r i", i=4),
                           in_=v_raw[g][:].rearrange("p h (r c i) -> p h c r i", r=PACK, i=4))
            return packed

        decay = {}

        def scale_mask(g, first, count, engine="scalar"):
            source, lo = mask_raw[g, first]
            cols = slice(lo, lo + QB * count)
            tile = kept("decay%d%d" % (g, first), [P, PACK, count * QB], F32)
            for r in range(PACK):
                if engine == "scalar":
                    nc.scalar.activation(out=tile[:, r, :], in_=source[:, r, cols], func=ACT.Copy,
                                         scale=t_sb[:, g, r : r + 1])
                elif engine == "vector":
                    nc.vector.tensor_scalar(out=tile[:, r, :], in0=source[:, r, cols], scalar1=t_sb[:, g, r : r + 1],
                                            scalar2=None, op0=ALU.mult)
                else:
                    nc.gpsimd.tensor_scalar(out=tile[:, r, :], in0=source[:, r, cols], scalar1=t_sb[:, g, r : r + 1],
                                            scalar2=0.0, op0=ALU.mult, op1=ALU.add)
            for b in range(count):
                decay[g, first + b] = tile[:, :, b * QB : (b + 1) * QB]

        k_packed = {}
        pending = []
        q_mx = {}
        k_mx = {}
        v_mx = {}
        w_mx = {}
        banks = {}
        w_packed = {}
        y_banks = {}
        inv_rms = {}

        def quantize_k(g, pair):
            k_mx[g, pair] = quantize("k%d%d" % (g, pair), k_packed[g, pair][:].rearrange("p r s j -> p (r s j)"), 2 * P)

        def unit(u):
            g, rest = divmod(u, BLOCKS * H)
            b, h = divmod(rest, H)
            return g, b, h

        def scores(u):
            g, b, h = unit(u)
            rows = slice(ROWS * h, ROWS * (h + 1))
            bank = psum.tile([P, PACK, QB], F32, name="scores%d" % h)
            q_codes, q_scales, q_cols = q_mx[b]
            for r in range(PACK):
                k_codes, k_scales = k_mx[g, r // 2]
                k_cols = slice(P * (r % 2), P * (r % 2 + 1))
                nc.tensor.matmul_mx(out=bank[:, r, :], lhsT=k_codes[rows, k_cols].bitcast(FP8X4),
                                    lhsT_scale=k_scales[rows, k_cols],
                                    rhs=q_codes[rows, q_cols].bitcast(FP8X4), rhs_scale=q_scales[rows, q_cols],
                                    start=True, stop=True)
            banks[u] = bank

        def weigh(u):
            g, b, h = unit(u)
            packed = work.tile([P, QB, PACK], BF16, name="w_packed", align_bytes=64, bufs=6)
            nc.vector.tensor_tensor(out=packed[:].rearrange("p (c i) r -> p c r i", i=2),
                                    in0=banks[u][:].rearrange("p r (c i) -> p c r i", i=2),
                                    in1=decay[g, b].rearrange("p r (c i) -> p c r i", i=2), op=ALU.mult)
            w_packed[u] = packed

        def quantize_w(u):
            w_mx[u] = quantize("w%d" % u, w_packed[u][:].rearrange("p q r -> p (q r)"), QB)

        totals = kept("totals", [P, H * BLOCKS], F32)
        inverse = kept("inverse", [P, H * BLOCKS], F32)
        y_tiles = [psum.tile([P, 3, E], F32, name="y", bufs=4) for bank in range(4)]

        def roots(lo, hi):
            nc.scalar.activation(out=inverse[:, lo:hi], in_=totals[:, lo:hi], func=ACT.Abs_reciprocal_sqrt,
                                 scale=1.0 / E, bias=256.0 * EPS)

        def read_values(u):
            last, b, h = unit(u)
            n = u - H * BLOCKS
            slot, bank = (0, H + h) if b == BLOCKS - 1 else (b, h)
            y = y_tiles[bank][:, slot, :]
            cols = slice(E * h, E * (h + 1))
            for g in range(PASSES):
                w_codes, w_scales = w_mx[u - (last - g) * BLOCKS * H]
                v_codes, v_scales = v_mx[g]
                nc.tensor.matmul_mx(out=y, lhsT=w_codes[:].bitcast(FP8X4), lhsT_scale=w_scales[:],
                                    rhs=v_codes[:, cols].bitcast(FP8X4), rhs_scale=v_scales[:, cols],
                                    start=(g == 0), stop=(g == last))
            y_banks[u] = y
            squares = work.tile([P, E], F32, name="squares")
            nc.scalar.activation(out=squares[:], in_=y, func=ACT.Square, accum_out=totals[:, n : n + 1])
            inv_rms[u] = inverse[:, n : n + 1]
            if n == ROOTS_FROM:
                roots(0, n)
            elif n > ROOTS_FROM:
                roots(n - 1, n)
            if u == UNITS - 1:
                roots(n, n + 1)

        gate = kept("gate", [P, H * BLOCKS, E], F32)
        gains = kept("gains", [P, H * BLOCKS, E], F32)

        def gain(engine, lo, count):
            tiles = slice(lo, lo + count)
            engine.tensor_tensor(out=gains[:, tiles, :], in0=gate[:, tiles, :],
                                 in1=gn_sb[:].unsqueeze(1).to_broadcast([P, count, E]), op=ALU.mult)

        def finish(u):
            last, b, h = unit(u)
            result = work.tile([P, E], F32, name="result", bufs=8)
            nc.vector.scalar_tensor_tensor(out=result[:], in0=y_banks[u], scalar=inv_rms[u],
                                           in1=gains[:, h * BLOCKS + b, :], op0=ALU.mult, op1=ALU.mult)
            nc.sync.dma_start(out=out_rows[:, h * BLOCKS + b, :], in_=result[:])

        nc.scalar.activation(out=gate[:, 0:1, :], in_=og_first[:], func=ACT.Sigmoid)
        pack_k(0, 0, "vector")
        pack_k(0, 1, "scalar")
        quantize_k(0, 0)
        quantize_k(0, 1)
        q_first = pack_q(0, 1, "vector")
        q_second = pack_q(1, 1, "vector")
        q_rest = pack_q(2, 2, "scalar")
        quantize_q(0, 1, q_first)
        quantize_q(1, 1, q_second)
        scale_mask(0, 0, 1, "vector")
        quantize_q(2, 2, q_rest)
        scale_mask(0, 1, 1)
        scale_mask(0, 2, 2)
        for h in range(H):
            lo = max(1, BLOCKS * h)
            hi = BLOCKS * (h + 1)
            nc.scalar.activation(out=gate[:, lo:hi, :], in_=og_rest[:, lo - 1 : hi - 1, :], func=ACT.Sigmoid)
            if h == 0:
                gain(nc.gpsimd, 0, BLOCKS)
        warm = kept("warm", [P, 1], F32)
        nc.scalar.activation(out=warm[:], in_=gate[:, 0, 0:1], func=ACT.Abs_reciprocal_sqrt)
        pack_k(1, 1, "scalar", 0, 64)
        scale_mask(1, 0, 1)
        scale_mask(1, 1, 1)
        v_packed = [pack_v(0), pack_v(1)]
        scale_mask(1, 2, 1)
        scale_mask(1, 3, 1)

        groups = {10: [8, 9, 10], 11: [11], 12: [12], 13: [13], 14: [14], 15: [15]}
        issued = 0
        ready = 8
        for s in range(UNITS + 1):
            while issued < min(s + 3, ready):
                scores(issued)
                issued = issued + 1
            if s < UNITS:
                weigh(s)
            else:
                gain(nc.vector, BLOCKS, 1)
            if s == 7:
                pack_k(1, 0, "vector")
                pack_k(1, 1, "vector", 64, P)
                quantize_k(1, 0)
                quantize_k(1, 1)
                ready = UNITS
                for u in range(3, 6):
                    quantize_w(u)
            for g in range(PASSES):
                if s == (10, 11)[g]:
                    v_mx[g] = quantize("v%d" % g, v_packed[g][:].rearrange("p h e r -> p (h e r)"), H * E)
            while issued < min(s + 4, ready):
                scores(issued)
                issued = issued + 1
            if s >= 1 and not 3 <= s - 1 < 6:
                quantize_w(s - 1)
            for u in groups.get(s - 1, []):
                read_values(u)
        for b in range(BLOCKS - 1):
            finish(UNITS // 2 + H * b)
            gain(nc.vector, BLOCKS + b + 1, 1)
        for u in (9, 11, 13, 14, 15):
            finish(u)
